import numpy as np
import ml_dtypes


def mxq(x, axis, fmt="e4m3"):
    dtype, down = {"e4m3": (ml_dtypes.float8_e4m3fn, 7), "e5m2": (ml_dtypes.float8_e5m2, 14)}[fmt]
    v = np.moveaxis(np.asarray(x, np.float32).astype(ml_dtypes.bfloat16).astype(np.float64), axis, -1)
    blocks = v.reshape(v.shape[:-1] + (-1, 32))
    amax = np.abs(blocks).max(-1, keepdims=True)
    byte = np.maximum(np.where(amax > 0, np.frexp(amax)[1] - 1 + 127, 0) - down, 1)
    scale = np.exp2(byte - 127.0)
    codes = (blocks / scale).astype(np.float32).astype(dtype).astype(np.float64)
    return np.moveaxis((codes * scale).reshape(v.shape), -1, axis)


WIDE = False


def mx_kscale(k):
    if not WIDE:
        return np.ones(k)
    levels = np.array([10, -10, 5, -5, 0])
    if k % 512:
        return np.exp2(np.random.permutation(np.resize(levels, k // 32))).repeat(32)
    a = np.empty((k // 512, 16))
    for p in range(k // 512):
        a[p, :8] = np.random.permutation(np.resize(levels, 8))
        for g in range(8):
            far = levels[np.abs(levels - a[p, g]) >= 10]
            a[p, g + 8] = far[np.random.randint(len(far))]
    return np.exp2(a.ravel()).repeat(32)


def f64(x):
    return np.asarray(x).astype(np.float64)


def striped(idx):
    return np.tile(idx.reshape(-1, 16).T, (8, 1)).astype(np.uint16)


def unstriped(offs):
    return offs[:16].T.reshape(-1).astype(np.int64)


def relu2(v):
    return np.maximum(v, 0.0) ** 2


K, T, E, C, N = 1024, 1024, 8, 256, 256


def by_expert(wq, xq):
    return np.concatenate([wq[e].T @ xq[:, e * C:(e + 1) * C] for e in range(E)], axis=1)


def setup_inputs():
    n = np.random.standard_normal
    s = mx_kscale(K)[:, None]
    first = np.random.permutation(np.repeat(np.arange(E), T // E))
    second = (first + 1 + np.random.permutation(np.repeat(np.arange(E - 1), -(-T // (E - 1)))[:T])) % E
    while np.bincount(second, minlength=E).max() != T // E:
        load = np.bincount(second, minlength=E); hi, lo = int(load.argmax()), int(load.argmin())
        t = np.flatnonzero((second == hi) & (first != lo))[0]; second[t] = lo
    slot_token = np.empty(E * C, np.int64); pos = np.empty((2, T), np.int64); fill = np.zeros(E, np.int64)
    place = np.stack([np.random.permutation(C) for _ in range(E)])
    for r, deal in enumerate((first, second)):
        for t in np.random.permutation(T):
            e = deal[t]; j = e * C + place[e, fill[e]]; fill[e] += 1; slot_token[j] = t; pos[r, t] = j
    g = np.random.uniform(0.2, 0.8, T)
    return {
        "xT": (n((K, T)) * s).astype(np.float32),
        "w": (n((E + 1, K, N)) / np.sqrt(K) / s[None]).astype(np.float32),
        "b": (0.3 * n((N, E + 1))).astype(np.float32),
        "gate": np.stack([np.tile(g, (N, 1)), np.tile(1.0 - g, (N, 1))]).astype(np.float32),
        "offs": striped(slot_token),
        "pos1": striped(pos[0]),
        "pos2": striped(pos[1]),
    }


def reference(xT, w, b, gate, offs, pos1, pos2):
    idx = unstriped(offs)
    wq = mxq(f64(w), 1, "e4m3")
    xs = mxq(f64(xT), 0, "e4m3")
    ys = relu2((wq[E].T @ xs) + f64(b)[:, E:])
    xq = mxq(f64(xT)[:, idx], 0, "e4m3")
    y = by_expert(wq, xq)
    y = relu2(y + np.repeat(f64(b)[:, :E], C, axis=1))
    return ys + f64(gate[0]) * y[:, unstriped(pos1)] + f64(gate[1]) * y[:, unstriped(pos2)]

@@ -1,0 +1,286 @@
+from contextlib import ExitStack
+
+import concourse.mybir as mybir
+
+K, T, E, C, N = 1024, 1024, 8, 256, 256
+S = E * C
+P = 128
+FLOPS = 2 * K * N * (S + T)
+
+F32 = mybir.dt.float32
+BF16 = mybir.dt.bfloat16
+U32 = mybir.dt.uint32
+U16 = mybir.dt.uint16
+U8 = mybir.dt.uint8
+FP8X4 = mybir.dt.float8_e4m3fn_x4
+
+RELU = mybir.ActivationFunctionType.Relu
+SQUARE = mybir.ActivationFunctionType.Square
+MULT, ADD = mybir.AluOpType.mult, mybir.AluOpType.add
+
+CHUNKS = ((0, 3), (3, 3), (6, 2))
+HALF = 512
+RAW_BUFS = 6
+WBF_BUFS = 4
+ON_GPSIMD = ()
+HEAD = (0, 512, 768, 1024)
+GROUP_S_ENGINE = ("v", "s", "v", "v")
+
+
+def tile_moe_shr_lin_relu2_kernel(tc, xT, w, b, gate, offs, pos1, pos2, out):
+    nc = tc.nc
+    with ExitStack() as ctx:
+        lists = ctx.enter_context(tc.tile_pool(name="lists", bufs=1))
+        keep = ctx.enter_context(tc.tile_pool(name="keep", bufs=1))
+        stage = ctx.enter_context(tc.tile_pool(name="stage", bufs=RAW_BUFS))
+        group = ctx.enter_context(tc.tile_pool(name="group", bufs=4))
+        comb = ctx.enter_context(tc.tile_pool(name="comb", bufs=3))
+        psum = ctx.enter_context(tc.psum_pool(name="psum", bufs=8))
+
+        offs_t = lists.tile([P, S // 16], U16, name="offs_t")
+        pos1_t = lists.tile([P, T // 16], U16, name="pos1_t")
+        pos2_t = lists.tile([P, T // 16], U16, name="pos2_t")
+        pos = (pos1_t, pos2_t)
+
+        bias = keep.tile([P, 2, E + 1], F32, name="bias")
+        planes = keep.tile([P, 4, T], U32, name="planes")
+        picked = [keep.tile([P, 4, n * C], U32, name=f"picked{i}") for i, (e0, n) in enumerate(CHUNKS)]
+        y = [keep.tile([P, S], F32, name=f"y{m}") for m in range(2)]
+        ys = [keep.tile([P, T], F32, name=f"ys{m}") for m in range(2)]
+        gates = [keep.tile([P, 2, T], F32, name=f"gate{m}") for m in range(2)]
+        wcodes = [keep.tile([P, 2 * N], U32, name=f"wcodes{e}", align_bytes=64) for e in range(E + 1)]
+        wscales = [keep.tile([P, 2 * N], U8, name=f"wscales{e}", align_bytes=64) for e in range(E + 1)]
+        xcodes, xscales = {}, {}
+        scodes = [keep.tile([P, 2, HALF], U32, name=f"scodes{h}", align_bytes=64) for h in range(2)]
+        sscales = [keep.tile([P, 2, HALF], U8, name=f"sscales{h}", align_bytes=64) for h in range(2)]
+
+        nc.scalar.dma_start(bias[:], b.rearrange("(m p) e -> p m e", p=P))
+
+        order = [("x", 0), ("x", 1), ("w", 0), ("x", 2), ("w", 1), ("x", 3)] + [("w", e) for e in range(2, E + 1)]
+        raw = {}
+
+        def load(i):
+            kind, j = order[i]
+            t = stage.tile([P, 2048], F32, name="raw")
+            raw[order[i]] = t
+            if kind == "x":
+                g, h = divmod(j, 2)
+                rows = xT[512 * g : 512 * (g + 1), :].rearrange("(p j) t -> p j t", j=4)[:, 2 * h : 2 * h + 2, :]
+                dst = t[:].rearrange("p (j t) -> p j t", j=2)
+                if j == 0:
+                    for c0, c1 in zip(HEAD[:-1], HEAD[1:]):
+                        nc.sync.dma_start(dst[:, :, c0:c1], rows[:, :, c0:c1])
+                        if c0 == 0:
+                            nc.sync.dma_start(offs_t[:], offs)
+                else:
+                    nc.sync.dma_start(dst, rows)
+            else:
+                nc.sync.dma_start(
+                    t[:].rearrange("p (g j n) -> p g j n", g=2, j=4),
+                    w[j].rearrange("(g p j) n -> p g j n", p=P, j=4),
+                )
+                if j == 2:
+                    nc.sync.dma_start(pos1_t[:], pos1)
+                    nc.sync.dma_start(pos2_t[:], pos2)
+                if j == E:
+                    for m in range(2):
+                        nc.sync.dma_start(gates[m][:], gate[:, m * P : (m + 1) * P, :].rearrange("r p t -> p r t"))
+
+        issued = [0]
+
+        def load_until(i):
+            while issued[0] < min(i, len(order)):
+                load(issued[0])
+                issued[0] += 1
+
+        def before_cast(unit):
+            load_until(order.index(unit) + RAW_BUFS)
+
+        def cast_plane(q):
+            before_cast(("x", q))
+            src = raw[("x", q)][:].rearrange("p (e t) -> p t e", e=2)
+            dst = planes[:, q, :].bitcast(BF16).rearrange("p (t e) -> p t e", e=2)
+            if q == 0:
+                for c0, c1 in zip(HEAD[:-1], HEAD[1:]):
+                    cols = slice(c0, c1)
+                    nc.vector.tensor_copy(dst[:, cols, :], src[:, cols, :])
+            else:
+                nc.scalar.copy(dst, src)
+
+        wbf = {}
+
+        def cast_w(e):
+            before_cast(("w", e))
+            t = group.tile([P, 2 * N * 4], BF16, name="wbf", align_bytes=64, bufs=WBF_BUFS)
+            wbf[e] = t
+            for g in range(2):
+                src = raw[("w", e)][:, 4 * N * g : 4 * N * (g + 1)].rearrange("p (j c i) -> p c j i", j=4, i=4)
+                dst = t[:, 4 * N * g : 4 * N * (g + 1)].rearrange("p (c i j) -> p c j i", i=4, j=4)
+                if e in ON_GPSIMD:
+                    nc.gpsimd.tensor_scalar(dst, src, 1.0, 0.0, MULT, ADD)
+                else:
+                    nc.scalar.copy(dst, src)
+
+        def quant_w(e):
+            nc.vector.quantize_mx(out=wcodes[e][:].bitcast(FP8X4), scales=wscales[e][:], in_=wbf[e][:])
+
+        def gather(q):
+            for i, (e0, n) in enumerate(CHUNKS):
+                nc.vector.tensor_copy(picked[i][:, q, :], planes[:, q, :].indirect(offs_t[:, 16 * e0 : 16 * (e0 + n)]))
+
+        xbf = {}
+
+        def group_x(e):
+            i = [k for k, (e0, n) in enumerate(CHUNKS) if e0 <= e < e0 + n][0]
+            c0 = (e - CHUNKS[i][0]) * C
+            t = group.tile([P, 2048], BF16, name="xbf", align_bytes=64)
+            xbf[e] = t
+            for g in range(2):
+                src = picked[i][:, 2 * g : 2 * g + 2, c0 : c0 + C].bitcast(BF16).rearrange("p h (c e) -> p c h e", e=2)
+                dst = t[:, 4 * C * g : 4 * C * (g + 1)].rearrange("p (c h e) -> p c h e", h=2, e=2)
+                nc.vector.tensor_copy(dst, src)
+
+        def quant_x(e):
+            xc = group.tile([P, 2 * C], U32, name="xc", align_bytes=64)
+            xs = group.tile([P, 2 * C], U8, name="xs", align_bytes=64)
+            xcodes[e], xscales[e] = xc, xs
+            nc.vector.quantize_mx(out=xcodes[e][:].bitcast(FP8X4), scales=xscales[e][:], in_=xbf[e][:])
+
+        def multiply(e):
+            ps = psum.tile([P, 2 * C], F32, name="ps")
+            for m in range(2):
+                for g in range(2):
+                    wc = slice(N * g + P * m, N * g + P * (m + 1))
+                    xc = slice(C * g, C * (g + 1))
+                    nc.tensor.matmul_mx(
+                        out=ps[:, C * m : C * (m + 1)],
+                        lhsT=wcodes[e][:, wc].bitcast(FP8X4),
+                        lhsT_scale=wscales[e][:, wc],
+                        rhs=xcodes[e][:, xc].bitcast(FP8X4),
+                        rhs_scale=xscales[e][:, xc],
+                        start=(g == 0),
+                        stop=(g == 1),
+                    )
+            return ps
+
+        def relu(e, ps, m):
+            nc.scalar.activation(y[m][:, C * e : C * (e + 1)], ps[:, C * m : C * (m + 1)], RELU, bias=bias[:, m, e : e + 1])
+
+        def square(e, m):
+            v = y[m][:, C * (e - 1) : C * (e + 1)]
+            nc.scalar.activation(v, v, SQUARE)
+
+        cast_plane(0)
+        cast_plane(1)
+        cast_w(0)
+        gather(0)
+        cast_plane(2)
+        cast_w(1)
+        gather(1)
+        cast_plane(3)
+        cast_w(2)
+        gather(2)
+        cast_w(3)
+        quant_w(0)
+        quant_w(1)
+        gather(3)
+
+        sbf = {}
+
+        def group_s(h, g):
+            t = group.tile([P, 2048], BF16, name="sbf", align_bytes=64, bufs=2)
+            sbf[(h, g)] = t
+            src = planes[:, 2 * g : 2 * g + 2, HALF * h : HALF * (h + 1)].bitcast(BF16).rearrange("p q (c e) -> p c q e", e=2)
+            dst = t[:].rearrange("p (c q e) -> p c q e", q=2, e=2)
+            if GROUP_S_ENGINE[2 * h + g] == "v":
+                nc.vector.tensor_copy(dst, src)
+            else:
+                nc.scalar.copy(dst, src)
+
+        def quant_s(h, g):
+            nc.vector.quantize_mx(out=scodes[h][:, g, :].bitcast(FP8X4), scales=sscales[h][:, g, :], in_=sbf[(h, g)][:])
+
+        def multiply_s(m, h):
+            ps = psum.tile([P, HALF], F32, name="ps")
+            for g in range(2):
+                wc = slice(N * g + P * m, N * g + P * (m + 1))
+                nc.tensor.matmul_mx(
+                    out=ps[:],
+                    lhsT=wcodes[E][:, wc].bitcast(FP8X4),
+                    lhsT_scale=wscales[E][:, wc],
+                    rhs=scodes[h][:, g, :].bitcast(FP8X4),
+                    rhs_scale=sscales[h][:, g, :],
+                    start=(g == 0),
+                    stop=(g == 1),
+                )
+            v = ys[m][:, HALF * h : HALF * (h + 1)]
+            nc.scalar.activation(v, ps[:], RELU, bias=bias[:, m, E : E + 1])
+            nc.scalar.activation(v, v, SQUARE)
+
+        units = [(m, h) for m in range(2) for h in range(2)]
+        part = {}
+
+        def fetch(u, r):
+            m, h = units[u]
+            t = comb.tile([P, HALF], F32, name=f"part{r}")
+            part[(u, r)] = t
+            nc.vector.tensor_tensor(
+                t[:],
+                y[m][:].indirect(pos[r][:, 32 * h : 32 * (h + 1)]),
+                gates[m][:, r, HALF * h : HALF * (h + 1)],
+                MULT,
+            )
+
+        def add_parts(u):
+            nc.vector.tensor_tensor(part[(u, 0)][:], part[(u, 0)][:], part[(u, 1)][:], ADD)
+
+        def finish(u):
+            m, h = units[u]
+            t = part[(u, 0)]
+            nc.vector.tensor_tensor(t[:], t[:], ys[m][:, HALF * h : HALF * (h + 1)], ADD)
+            nc.sync.dma_start(out[m * P : (m + 1) * P, HALF * h : HALF * (h + 1)], t[:])
+
+        group_x(0)
+        for e in range(E):
+            if e >= 2:
+                quant_w(e)
+            if e + 1 < E:
+                group_x(e + 1)
+            if e + 4 <= E:
+                cast_w(e + 4)
+            quant_x(e)
+            ps = multiply(e)
+            for m in range(2):
+                relu(e, ps, m)
+                if e % 2 == 1:
+                    square(e, m)
+            if e >= E - 2:
+                group_s(0, e - E + 2)
+
+        quant_w(E)
+        fetch(0, 0)
+        fetch(0, 1)
+        fetch(1, 0)
+        add_parts(0)
+        fetch(1, 1)
+        quant_s(0, 0)
+        add_parts(1)
+        quant_s(0, 1)
+        multiply_s(0, 0)
+        multiply_s(1, 0)
+        group_s(1, 0)
+        group_s(1, 1)
+        fetch(2, 0)
+        quant_s(1, 0)
+        quant_s(1, 1)
+        multiply_s(0, 1)
+        multiply_s(1, 1)
+        fetch(2, 1)
+        finish(0)
+        fetch(3, 0)
+        add_parts(2)
+        fetch(3, 1)
+        finish(1)
+        finish(2)
+        add_parts(3)
+        finish(3)

@@ -20,11 +20,9 @@ MULT, ADD = mybir.AluOpType.mult, mybir.AluOpType.add
 
 CHUNKS = ((0, 3), (3, 3), (6, 2))
 HALF = 512
-RAW_BUFS = 6
-WBF_BUFS = 4
-ON_GPSIMD = ()
-HEAD = (0, 512, 768, 1024)
-GROUP_S_ENGINE = ("v", "s", "v", "v")
+RAW_BUFS = 8
+AHEAD = 6
+UNITS = ((0, 0, 1024), (1, 0, 512), (1, 512, 1024))
 
 
 def tile_moe_shr_lin_relu2_kernel(tc, xT, w, b, gate, offs, pos1, pos2, out):
@@ -33,8 +31,7 @@ def tile_moe_shr_lin_relu2_kernel(tc, xT, w, b, gate, offs, pos1, pos2, out):
         lists = ctx.enter_context(tc.tile_pool(name="lists", bufs=1))
         keep = ctx.enter_context(tc.tile_pool(name="keep", bufs=1))
         stage = ctx.enter_context(tc.tile_pool(name="stage", bufs=RAW_BUFS))
-        group = ctx.enter_context(tc.tile_pool(name="group", bufs=4))
-        comb = ctx.enter_context(tc.tile_pool(name="comb", bufs=3))
+        group = ctx.enter_context(tc.tile_pool(name="group", bufs=1))
         psum = ctx.enter_context(tc.psum_pool(name="psum", bufs=8))
 
         offs_t = lists.tile([P, S // 16], U16, name="offs_t")
@@ -43,173 +40,171 @@ def tile_moe_shr_lin_relu2_kernel(tc, xT, w, b, gate, offs, pos1, pos2, out):
         pos = (pos1_t, pos2_t)
 
         bias = keep.tile([P, 2, E + 1], F32, name="bias")
-        planes = keep.tile([P, 4, T], U32, name="planes")
+        plane0 = keep.tile([P, T], U32, name="plane0")
+        plane1 = keep.tile([P, T], U32, name="plane1")
+        planes23 = keep.tile([P, 2, T], U32, name="planes23")
+        planes = (plane0[:], plane1[:], planes23[:, 0, :], planes23[:, 1, :])
         picked = [keep.tile([P, 4, n * C], U32, name=f"picked{i}") for i, (e0, n) in enumerate(CHUNKS)]
         y = [keep.tile([P, S], F32, name=f"y{m}") for m in range(2)]
         ys = [keep.tile([P, T], F32, name=f"ys{m}") for m in range(2)]
-        gates = [keep.tile([P, 2, T], F32, name=f"gate{m}") for m in range(2)]
-        wcodes = [keep.tile([P, 2 * N], U32, name=f"wcodes{e}", align_bytes=64) for e in range(E + 1)]
-        wscales = [keep.tile([P, 2 * N], U8, name=f"wscales{e}", align_bytes=64) for e in range(E + 1)]
-        xcodes, xscales = {}, {}
-        scodes = [keep.tile([P, 2, HALF], U32, name=f"scodes{h}", align_bytes=64) for h in range(2)]
-        sscales = [keep.tile([P, 2, HALF], U8, name=f"sscales{h}", align_bytes=64) for h in range(2)]
+        wcodes = [keep.tile([P, 4 * N], U32, name=f"wcodes{k}", align_bytes=64) for k in range(E // 2)]
+        wscales = [keep.tile([P, 4 * N], U8, name=f"wscales{k}", align_bytes=64) for k in range(E // 2)]
+        wcodes.append(keep.tile([P, 2 * N], U32, name="wcodes8", align_bytes=64))
+        wscales.append(keep.tile([P, 2 * N], U8, name="wscales8", align_bytes=64))
+        scodes = [keep.tile([P, T], U32, name=f"scodes{g}", align_bytes=64) for g in range(2)]
+        sscales = [keep.tile([P, T], U8, name=f"sscales{g}", align_bytes=64) for g in range(2)]
 
-        nc.scalar.dma_start(bias[:], b.rearrange("(m p) e -> p m e", p=P))
+        nc.sync.dma_start(offs_t[:], offs)
+        rows = [xT[HALF * g : HALF * (g + 1), :].rearrange("(p j) t -> p j t", j=4) for g in range(2)]
+        raw01 = []
+        for h in range(2):
+            t = stage.tile([P, 2048], F32, name="raw")
+            raw01.append(t[:].rearrange("p (j t) -> p j t", j=4))
+        for q in range(2):
+            for h in range(2):
+                cols = slice(h * HALF, (h + 1) * HALF)
+                nc.sync.dma_start(raw01[h][:, 2 * q : 2 * q + 2, :], rows[0][:, 2 * q : 2 * q + 2, cols])
 
-        order = [("x", 0), ("x", 1), ("w", 0), ("x", 2), ("w", 1), ("x", 3)] + [("w", e) for e in range(2, E + 1)]
+        ring = [("x", 2), ("x", 3)] + [("w", e) for e in range(E + 1)] + [("gate", 0), ("gate", 1)]
         raw = {}
 
-        def load(i):
-            kind, j = order[i]
+        def load(unit):
+            kind, j = unit
             t = stage.tile([P, 2048], F32, name="raw")
-            raw[order[i]] = t
+            raw[unit] = t
             if kind == "x":
-                g, h = divmod(j, 2)
-                rows = xT[512 * g : 512 * (g + 1), :].rearrange("(p j) t -> p j t", j=4)[:, 2 * h : 2 * h + 2, :]
-                dst = t[:].rearrange("p (j t) -> p j t", j=2)
-                if j == 0:
-                    for c0, c1 in zip(HEAD[:-1], HEAD[1:]):
-                        nc.sync.dma_start(dst[:, :, c0:c1], rows[:, :, c0:c1])
-                        if c0 == 0:
-                            nc.sync.dma_start(offs_t[:], offs)
-                else:
-                    nc.sync.dma_start(dst, rows)
-            else:
+                nc.sync.dma_start(t[:].rearrange("p (j t) -> p j t", j=2), rows[1][:, 2 * j - 4 : 2 * j - 2, :])
+            elif kind == "w":
                 nc.sync.dma_start(
                     t[:].rearrange("p (g j n) -> p g j n", g=2, j=4),
                     w[j].rearrange("(g p j) n -> p g j n", p=P, j=4),
                 )
-                if j == 2:
-                    nc.sync.dma_start(pos1_t[:], pos1)
-                    nc.sync.dma_start(pos2_t[:], pos2)
-                if j == E:
-                    for m in range(2):
-                        nc.sync.dma_start(gates[m][:], gate[:, m * P : (m + 1) * P, :].rearrange("r p t -> p r t"))
+            else:
+                nc.sync.dma_start(
+                    t[:].rearrange("p (r t) -> p r t", r=2),
+                    gate[:, j * P : (j + 1) * P, :].rearrange("r p t -> p r t"),
+                )
+            if unit == ("w", E):
+                nc.sync.dma_start(bias[:], b.rearrange("(m p) e -> p m e", p=P))
+            if unit == ("w", 2):
+                nc.sync.dma_start(pos1_t[:], pos1)
+                nc.sync.dma_start(pos2_t[:], pos2)
 
-        issued = [0]
-
-        def load_until(i):
-            while issued[0] < min(i, len(order)):
-                load(issued[0])
-                issued[0] += 1
-
-        def before_cast(unit):
-            load_until(order.index(unit) + RAW_BUFS)
+        def load_ahead(unit):
+            for u in ring[: ring.index(unit) + AHEAD]:
+                if u not in raw:
+                    load(u)
 
         def cast_plane(q):
-            before_cast(("x", q))
-            src = raw[("x", q)][:].rearrange("p (e t) -> p t e", e=2)
-            dst = planes[:, q, :].bitcast(BF16).rearrange("p (t e) -> p t e", e=2)
-            if q == 0:
-                for c0, c1 in zip(HEAD[:-1], HEAD[1:]):
-                    cols = slice(c0, c1)
-                    nc.vector.tensor_copy(dst[:, cols, :], src[:, cols, :])
+            dst = planes[q].bitcast(BF16).rearrange("p (t e) -> p t e", e=2)
+            if q < 2:
+                for h in range(2):
+                    half = dst[:, h * HALF : (h + 1) * HALF, :]
+                    src = raw01[h][:, 2 * q : 2 * q + 2, :].rearrange("p e t -> p t e")
+                    if q == 0:
+                        nc.vector.tensor_copy(half, src)
+                    else:
+                        nc.scalar.copy(half, src)
             else:
-                nc.scalar.copy(dst, src)
+                load_ahead(("x", q))
+                nc.scalar.copy(dst, raw[("x", q)][:].rearrange("p (e t) -> p t e", e=2))
 
         wbf = {}
 
         def cast_w(e):
-            before_cast(("w", e))
-            t = group.tile([P, 2 * N * 4], BF16, name="wbf", align_bytes=64, bufs=WBF_BUFS)
-            wbf[e] = t
+            load_ahead(("w", e))
+            if e % 2 == 0:
+                t = group.tile([P, 16 * N], BF16, name="wbf", align_bytes=64, bufs=4)
+                wbf[e // 2] = t
             for g in range(2):
                 src = raw[("w", e)][:, 4 * N * g : 4 * N * (g + 1)].rearrange("p (j c i) -> p c j i", j=4, i=4)
-                dst = t[:, 4 * N * g : 4 * N * (g + 1)].rearrange("p (c i j) -> p c j i", i=4, j=4)
-                if e in ON_GPSIMD:
-                    nc.gpsimd.tensor_scalar(dst, src, 1.0, 0.0, MULT, ADD)
-                else:
-                    nc.scalar.copy(dst, src)
+                c0 = 8 * N * (e % 2) + 4 * N * g
+                dst = wbf[e // 2][:, c0 : c0 + 4 * N].rearrange("p (c i j) -> p c j i", i=4, j=4)
+                nc.scalar.copy(dst, src)
 
-        def quant_w(e):
-            nc.vector.quantize_mx(out=wcodes[e][:].bitcast(FP8X4), scales=wscales[e][:], in_=wbf[e][:])
+        def quant_w(k):
+            n = 4 * N if k < E // 2 else 2 * N
+            nc.vector.quantize_mx(out=wcodes[k][:].bitcast(FP8X4), scales=wscales[k][:], in_=wbf[k][:, 0 : 4 * n])
 
-        def gather(q):
-            for i, (e0, n) in enumerate(CHUNKS):
-                nc.vector.tensor_copy(picked[i][:, q, :], planes[:, q, :].indirect(offs_t[:, 16 * e0 : 16 * (e0 + n)]))
+        def gather(q, chunks=(0, 1, 2)):
+            for i in chunks:
+                e0, n = CHUNKS[i]
+                nc.vector.tensor_copy(picked[i][:, q, :], planes[q].indirect(offs_t[:, 16 * e0 : 16 * (e0 + n)]))
 
-        xbf = {}
+        xbf, xcodes, xscales = {}, {}, {}
 
-        def group_x(e):
-            i = [k for k, (e0, n) in enumerate(CHUNKS) if e0 <= e < e0 + n][0]
-            c0 = (e - CHUNKS[i][0]) * C
-            t = group.tile([P, 2048], BF16, name="xbf", align_bytes=64)
-            xbf[e] = t
-            for g in range(2):
-                src = picked[i][:, 2 * g : 2 * g + 2, c0 : c0 + C].bitcast(BF16).rearrange("p h (c e) -> p c h e", e=2)
-                dst = t[:, 4 * C * g : 4 * C * (g + 1)].rearrange("p (c h e) -> p c h e", h=2, e=2)
-                nc.vector.tensor_copy(dst, src)
+        def group_x(i, g):
+            n = CHUNKS[i][1] * C
+            if g == 0:
+                t = group.tile([P, 8 * n], BF16, name="xbf", align_bytes=64)
+                xbf[i] = t
+            src = picked[i][:, 2 * g : 2 * g + 2, :].bitcast(BF16).rearrange("p h (c e) -> p c h e", e=2)
+            nc.vector.tensor_copy(xbf[i][:, 4 * n * g : 4 * n * (g + 1)].rearrange("p (c h e) -> p c h e", h=2, e=2), src)
 
-        def quant_x(e):
-            xc = group.tile([P, 2 * C], U32, name="xc", align_bytes=64)
-            xs = group.tile([P, 2 * C], U8, name="xs", align_bytes=64)
-            xcodes[e], xscales[e] = xc, xs
-            nc.vector.quantize_mx(out=xcodes[e][:].bitcast(FP8X4), scales=xscales[e][:], in_=xbf[e][:])
+        def quant_x(i):
+            n = CHUNKS[i][1] * C
+            xc = group.tile([P, 2 * n], U32, name="xc", align_bytes=64, bufs=2)
+            xs = group.tile([P, 2 * n], U8, name="xs", align_bytes=64, bufs=2)
+            xcodes[i], xscales[i] = xc, xs
+            for c0 in range(0, 2 * n, 1024):
+                c1 = min(c0 + 1024, 2 * n)
+                nc.vector.quantize_mx(out=xc[:, c0:c1].bitcast(FP8X4), scales=xs[:, c0:c1], in_=xbf[i][:, 4 * c0 : 4 * c1])
+
+        banks = {}
 
         def multiply(e):
+            i = [k for k, (e0, n) in enumerate(CHUNKS) if e0 <= e < e0 + n][0]
+            e0, n = CHUNKS[i]
             ps = psum.tile([P, 2 * C], F32, name="ps")
+            banks[e] = ps
             for m in range(2):
                 for g in range(2):
-                    wc = slice(N * g + P * m, N * g + P * (m + 1))
-                    xc = slice(C * g, C * (g + 1))
+                    w0 = 2 * N * (e % 2) + N * g + P * m
+                    x0 = C * (n * g + e - e0)
                     nc.tensor.matmul_mx(
                         out=ps[:, C * m : C * (m + 1)],
-                        lhsT=wcodes[e][:, wc].bitcast(FP8X4),
-                        lhsT_scale=wscales[e][:, wc],
-                        rhs=xcodes[e][:, xc].bitcast(FP8X4),
-                        rhs_scale=xscales[e][:, xc],
+                        lhsT=wcodes[e // 2][:, w0 : w0 + P].bitcast(FP8X4),
+                        lhsT_scale=wscales[e // 2][:, w0 : w0 + P],
+                        rhs=xcodes[i][:, x0 : x0 + C].bitcast(FP8X4),
+                        rhs_scale=xscales[i][:, x0 : x0 + C],
                         start=(g == 0),
                         stop=(g == 1),
                     )
-            return ps
 
-        def relu(e, ps, m):
-            nc.scalar.activation(y[m][:, C * e : C * (e + 1)], ps[:, C * m : C * (m + 1)], RELU, bias=bias[:, m, e : e + 1])
-
-        def square(e, m):
-            v = y[m][:, C * (e - 1) : C * (e + 1)]
+        def activate(k, m):
+            for e in (2 * k, 2 * k + 1):
+                v = y[m][:, C * e : C * (e + 1)]
+                nc.scalar.activation(v, banks[e][:, C * m : C * (m + 1)], RELU, bias=bias[:, m, e : e + 1])
+            v = y[m][:, 2 * C * k : 2 * C * (k + 1)]
             nc.scalar.activation(v, v, SQUARE)
-
-        cast_plane(0)
-        cast_plane(1)
-        cast_w(0)
-        gather(0)
-        cast_plane(2)
-        cast_w(1)
-        gather(1)
-        cast_plane(3)
-        cast_w(2)
-        gather(2)
-        cast_w(3)
-        quant_w(0)
-        quant_w(1)
-        gather(3)
 
         sbf = {}
 
-        def group_s(h, g):
-            t = group.tile([P, 2048], BF16, name="sbf", align_bytes=64, bufs=2)
-            sbf[(h, g)] = t
-            src = planes[:, 2 * g : 2 * g + 2, HALF * h : HALF * (h + 1)].bitcast(BF16).rearrange("p q (c e) -> p c q e", e=2)
-            dst = t[:].rearrange("p (c q e) -> p c q e", q=2, e=2)
-            if GROUP_S_ENGINE[2 * h + g] == "v":
-                nc.vector.tensor_copy(dst, src)
+        def group_s(g, h=0):
+            if g == 0:
+                t = group.tile([P, 4 * HALF], BF16, name="sbf", align_bytes=64, bufs=2)
+                src = raw01[h].rearrange("p j (c i) -> p c j i", i=4)
+                nc.scalar.copy(t[:].rearrange("p (c i j) -> p c j i", i=4, j=4), src)
             else:
-                nc.scalar.copy(dst, src)
+                t = group.tile([P, 4 * T], BF16, name="xbf", align_bytes=64)
+                src = planes23[:].bitcast(BF16).rearrange("p q (c e) -> p c q e", e=2)
+                nc.vector.tensor_copy(t[:].rearrange("p (c q e) -> p c q e", q=2, e=2), src)
+            sbf[(g, h)] = t
 
-        def quant_s(h, g):
-            nc.vector.quantize_mx(out=scodes[h][:, g, :].bitcast(FP8X4), scales=sscales[h][:, g, :], in_=sbf[(h, g)][:])
+        def quant_s(g, h=0):
+            cols = slice(h * HALF, (h + 1) * HALF) if g == 0 else slice(0, T)
+            nc.vector.quantize_mx(out=scodes[g][:, cols].bitcast(FP8X4), scales=sscales[g][:, cols], in_=sbf[(g, h)][:])
 
-        def multiply_s(m, h):
+        def shared(m, h):
             ps = psum.tile([P, HALF], F32, name="ps")
             for g in range(2):
-                wc = slice(N * g + P * m, N * g + P * (m + 1))
+                w0 = N * g + P * m
                 nc.tensor.matmul_mx(
                     out=ps[:],
-                    lhsT=wcodes[E][:, wc].bitcast(FP8X4),
-                    lhsT_scale=wscales[E][:, wc],
-                    rhs=scodes[h][:, g, :].bitcast(FP8X4),
-                    rhs_scale=sscales[h][:, g, :],
+                    lhsT=wcodes[E // 2][:, w0 : w0 + P].bitcast(FP8X4),
+                    lhsT_scale=wscales[E // 2][:, w0 : w0 + P],
+                    rhs=scodes[g][:, HALF * h : HALF * (h + 1)].bitcast(FP8X4),
+                    rhs_scale=sscales[g][:, HALF * h : HALF * (h + 1)],
                     start=(g == 0),
                     stop=(g == 1),
                 )
@@ -217,70 +212,92 @@ def tile_moe_shr_lin_relu2_kernel(tc, xT, w, b, gate, offs, pos1, pos2, out):
             nc.scalar.activation(v, ps[:], RELU, bias=bias[:, m, E : E + 1])
             nc.scalar.activation(v, v, SQUARE)
 
-        units = [(m, h) for m in range(2) for h in range(2)]
         part = {}
 
         def fetch(u, r):
-            m, h = units[u]
-            t = comb.tile([P, HALF], F32, name=f"part{r}")
-            part[(u, r)] = t
+            m, c0, c1 = UNITS[u]
+            if r == 0:
+                t = stage.tile([P, 2048], F32, name="raw")
+                part[u] = t[:].rearrange("p (r c) -> p r c", r=2)
+            weight = raw[("gate", m)][:, T * r + c0 : T * r + c1]
             nc.vector.tensor_tensor(
-                t[:],
-                y[m][:].indirect(pos[r][:, 32 * h : 32 * (h + 1)]),
-                gates[m][:, r, HALF * h : HALF * (h + 1)],
-                MULT,
+                part[u][:, r, 0 : c1 - c0], y[m][:].indirect(pos[r][:, c0 // 16 : c1 // 16]), weight, MULT
             )
 
         def add_parts(u):
-            nc.vector.tensor_tensor(part[(u, 0)][:], part[(u, 0)][:], part[(u, 1)][:], ADD)
+            m, c0, c1 = UNITS[u]
+            v = part[u][:, :, 0 : c1 - c0]
+            nc.vector.tensor_tensor(v[:, 0], v[:, 0], v[:, 1], ADD)
 
         def finish(u):
-            m, h = units[u]
-            t = part[(u, 0)]
-            nc.vector.tensor_tensor(t[:], t[:], ys[m][:, HALF * h : HALF * (h + 1)], ADD)
-            nc.sync.dma_start(out[m * P : (m + 1) * P, HALF * h : HALF * (h + 1)], t[:])
+            m, c0, c1 = UNITS[u]
+            v = part[u][:, 0, 0 : c1 - c0]
+            nc.vector.tensor_tensor(v, v, ys[m][:, c0:c1], ADD)
+            nc.sync.dma_start(out[m * P : (m + 1) * P, c0:c1], v)
 
-        group_x(0)
-        for e in range(E):
-            if e >= 2:
-                quant_w(e)
-            if e + 1 < E:
-                group_x(e + 1)
-            if e + 4 <= E:
-                cast_w(e + 4)
-            quant_x(e)
-            ps = multiply(e)
-            for m in range(2):
-                relu(e, ps, m)
-                if e % 2 == 1:
-                    square(e, m)
-            if e >= E - 2:
-                group_s(0, e - E + 2)
-
-        quant_w(E)
+        cast_plane(0)
+        cast_plane(1)
+        group_s(0, 0)
+        gather(0)
+        cast_plane(2)
+        cast_plane(3)
+        group_s(0, 1)
+        cast_w(0)
+        gather(1)
+        cast_w(1)
+        gather(2)
+        cast_w(2)
+        gather(3)
+        for e in range(3, E):
+            cast_w(e)
+        group_x(0, 0)
+        group_x(0, 1)
+        quant_s(0, 0)
+        quant_x(0)
+        group_x(1, 0)
+        quant_s(0, 1)
+        group_x(1, 1)
+        quant_w(0)
+        cast_w(E)
+        load_ahead(ring[-1])
+        quant_x(1)
+        multiply(0)
+        multiply(1)
+        activate(0, 0)
+        quant_w(1)
+        multiply(2)
+        multiply(3)
+        activate(1, 0)
+        activate(0, 1)
+        quant_w(2)
+        multiply(4)
+        multiply(5)
+        activate(2, 0)
+        activate(1, 1)
+        group_x(2, 0)
+        group_x(2, 1)
+        quant_w(3)
+        quant_x(2)
+        multiply(6)
+        multiply(7)
+        activate(3, 0)
+        activate(2, 1)
+        activate(3, 1)
+        group_s(1)
+        quant_w(4)
         fetch(0, 0)
+        quant_s(1)
         fetch(0, 1)
+        for m in range(2):
+            for h in range(2):
+                shared(m, h)
         fetch(1, 0)
         add_parts(0)
         fetch(1, 1)
-        quant_s(0, 0)
-        add_parts(1)
-        quant_s(0, 1)
-        multiply_s(0, 0)
-        multiply_s(1, 0)
-        group_s(1, 0)
-        group_s(1, 1)
-        fetch(2, 0)
-        quant_s(1, 0)
-        quant_s(1, 1)
-        multiply_s(0, 1)
-        multiply_s(1, 1)
-        fetch(2, 1)
         finish(0)
-        fetch(3, 0)
-        add_parts(2)
-        fetch(3, 1)
+        fetch(2, 0)
+        add_parts(1)
+        fetch(2, 1)
         finish(1)
+        add_parts(2)
         finish(2)
-        add_parts(3)
-        finish(3)

@@ -22,7 +22,7 @@ CHUNKS = ((0, 3), (3, 3), (6, 2))
 HALF = 512
 RAW_BUFS = 8
 AHEAD = 6
-UNITS = ((0, 0, 1024), (1, 0, 512), (1, 512, 1024))
+UNITS = ((0, 0, 1024), (1, 0, 640), (1, 640, 1024))
 
 
 def tile_moe_shr_lin_relu2_kernel(tc, xT, w, b, gate, offs, pos1, pos2, out):
@@ -171,10 +171,12 @@ def tile_moe_shr_lin_relu2_kernel(tc, xT, w, b, gate, offs, pos1, pos2, out):
                         stop=(g == 1),
                     )
 
-        def activate(k, m):
+        def relu(k, m):
             for e in (2 * k, 2 * k + 1):
                 v = y[m][:, C * e : C * (e + 1)]
                 nc.scalar.activation(v, banks[e][:, C * m : C * (m + 1)], RELU, bias=bias[:, m, e : e + 1])
+
+        def square(k, m):
             v = y[m][:, 2 * C * k : 2 * C * (k + 1)]
             nc.scalar.activation(v, v, SQUARE)
 
@@ -184,7 +186,8 @@ def tile_moe_shr_lin_relu2_kernel(tc, xT, w, b, gate, offs, pos1, pos2, out):
             if g == 0:
                 t = group.tile([P, 4 * HALF], BF16, name="sbf", align_bytes=64, bufs=2)
                 src = raw01[h].rearrange("p j (c i) -> p c j i", i=4)
-                nc.scalar.copy(t[:].rearrange("p (c i j) -> p c j i", i=4, j=4), src)
+                dst = t[:].rearrange("p (c i j) -> p c j i", i=4, j=4)
+                nc.scalar.copy(dst, src)
             else:
                 t = group.tile([P, 4 * T], BF16, name="xbf", align_bytes=64)
                 src = planes23[:].bitcast(BF16).rearrange("p q (c e) -> p c q e", e=2)
@@ -210,6 +213,9 @@ def tile_moe_shr_lin_relu2_kernel(tc, xT, w, b, gate, offs, pos1, pos2, out):
                 )
             v = ys[m][:, HALF * h : HALF * (h + 1)]
             nc.scalar.activation(v, ps[:], RELU, bias=bias[:, m, E : E + 1])
+
+        def square_shared(m, h):
+            v = ys[m][:, HALF * h : HALF * (h + 1)]
             nc.scalar.activation(v, v, SQUARE)
 
         part = {}
@@ -263,36 +269,46 @@ def tile_moe_shr_lin_relu2_kernel(tc, xT, w, b, gate, offs, pos1, pos2, out):
         quant_x(1)
         multiply(0)
         multiply(1)
-        activate(0, 0)
+        relu(0, 0)
         quant_w(1)
         multiply(2)
         multiply(3)
-        activate(1, 0)
-        activate(0, 1)
+        relu(1, 0)
+        square(0, 0)
         quant_w(2)
         multiply(4)
         multiply(5)
-        activate(2, 0)
-        activate(1, 1)
+        relu(2, 0)
+        square(1, 0)
+        square(2, 0)
         group_x(2, 0)
         group_x(2, 1)
         quant_w(3)
         quant_x(2)
         multiply(6)
         multiply(7)
-        activate(3, 0)
-        activate(2, 1)
-        activate(3, 1)
+        relu(3, 0)
+        square(3, 0)
+        relu(0, 1)
+        relu(1, 1)
+        square(0, 1)
+        relu(2, 1)
+        square(1, 1)
+        relu(3, 1)
+        square(2, 1)
+        square(3, 1)
         group_s(1)
         quant_w(4)
         fetch(0, 0)
         quant_s(1)
         fetch(0, 1)
         for m in range(2):
-            for h in range(2):
-                shared(m, h)
-        fetch(1, 0)
+            shared(m, 0)
+            shared(m, 1)
+            square_shared(m, 0)
+            square_shared(m, 1)
         add_parts(0)
+        fetch(1, 0)
         fetch(1, 1)
         finish(0)
         fetch(2, 0)

@@ -113,8 +113,12 @@ def tile_moe_shr_lin_relu2_kernel(tc, xT, w, b, gate, offs, pos1, pos2, out):
 
         def cast_w(e):
             load_ahead(("w", e))
-            if e % 2 == 0:
-                t = group.tile([P, 16 * N], BF16, name="wbf", align_bytes=64, bufs=4)
+            if e in (6, 7):
+                if e == 6:
+                    t = group.tile([P, 16 * N], BF16, name="tail", align_bytes=64)
+                    wbf[3] = t
+            elif e % 2 == 0:
+                t = group.tile([P, 16 * N], BF16, name="wbf", align_bytes=64, bufs=3)
                 wbf[e // 2] = t
             for g in range(2):
                 src = raw[("w", e)][:, 4 * N * g : 4 * N * (g + 1)].rearrange("p (j c i) -> p c j i", j=4, i=4)
@@ -152,24 +156,26 @@ def tile_moe_shr_lin_relu2_kernel(tc, xT, w, b, gate, offs, pos1, pos2, out):
 
         banks = {}
 
-        def multiply(e):
-            i = [k for k, (e0, n) in enumerate(CHUNKS) if e0 <= e < e0 + n][0]
-            e0, n = CHUNKS[i]
-            ps = psum.tile([P, 2 * C], F32, name="ps")
-            banks[e] = ps
+        def multiply(k):
+            for e in (2 * k, 2 * k + 1):
+                ps = psum.tile([P, 2 * C], F32, name="ps")
+                banks[e] = ps
             for m in range(2):
-                for g in range(2):
-                    w0 = 2 * N * (e % 2) + N * g + P * m
-                    x0 = C * (n * g + e - e0)
-                    nc.tensor.matmul_mx(
-                        out=ps[:, C * m : C * (m + 1)],
-                        lhsT=wcodes[e // 2][:, w0 : w0 + P].bitcast(FP8X4),
-                        lhsT_scale=wscales[e // 2][:, w0 : w0 + P],
-                        rhs=xcodes[i][:, x0 : x0 + C].bitcast(FP8X4),
-                        rhs_scale=xscales[i][:, x0 : x0 + C],
-                        start=(g == 0),
-                        stop=(g == 1),
-                    )
+                for e in (2 * k, 2 * k + 1):
+                    i = min(e // 3, 2)
+                    e0, n = CHUNKS[i]
+                    for g in range(2):
+                        w0 = 2 * N * (e % 2) + N * g + P * m
+                        x0 = C * (n * g + e - e0)
+                        nc.tensor.matmul_mx(
+                            out=banks[e][:, C * m : C * (m + 1)],
+                            lhsT=wcodes[k][:, w0 : w0 + P].bitcast(FP8X4),
+                            lhsT_scale=wscales[k][:, w0 : w0 + P],
+                            rhs=xcodes[i][:, x0 : x0 + C].bitcast(FP8X4),
+                            rhs_scale=xscales[i][:, x0 : x0 + C],
+                            start=(g == 0),
+                            stop=(g == 1),
+                        )
 
         def relu(k, m):
             for e in (2 * k, 2 * k + 1):
@@ -189,7 +195,7 @@ def tile_moe_shr_lin_relu2_kernel(tc, xT, w, b, gate, offs, pos1, pos2, out):
                 dst = t[:].rearrange("p (c i j) -> p c j i", i=4, j=4)
                 nc.scalar.copy(dst, src)
             else:
-                t = group.tile([P, 4 * T], BF16, name="xbf", align_bytes=64)
+                t = group.tile([P, 4 * T], BF16, name="tail", align_bytes=64)
                 src = planes23[:].bitcast(BF16).rearrange("p q (c e) -> p c q e", e=2)
                 nc.vector.tensor_copy(t[:].rearrange("p (c q e) -> p c q e", q=2, e=2), src)
             sbf[(g, h)] = t
@@ -268,16 +274,13 @@ def tile_moe_shr_lin_relu2_kernel(tc, xT, w, b, gate, offs, pos1, pos2, out):
         load_ahead(ring[-1])
         quant_x(1)
         multiply(0)
-        multiply(1)
         relu(0, 0)
         quant_w(1)
-        multiply(2)
-        multiply(3)
+        multiply(1)
         relu(1, 0)
         square(0, 0)
         quant_w(2)
-        multiply(4)
-        multiply(5)
+        multiply(2)
         relu(2, 0)
         square(1, 0)
         square(2, 0)
@@ -285,8 +288,7 @@ def tile_moe_shr_lin_relu2_kernel(tc, xT, w, b, gate, offs, pos1, pos2, out):
         group_x(2, 1)
         quant_w(3)
         quant_x(2)
-        multiply(6)
-        multiply(7)
+        multiply(3)
         relu(3, 0)
         square(3, 0)
         relu(0, 1)

from contextlib import ExitStack

import concourse.mybir as mybir

K, T, E, C, N = 1024, 1024, 8, 256, 256
S = E * C
P = 128
FLOPS = 2 * K * N * (S + T)

F32 = mybir.dt.float32
BF16 = mybir.dt.bfloat16
U32 = mybir.dt.uint32
U16 = mybir.dt.uint16
U8 = mybir.dt.uint8
FP8X4 = mybir.dt.float8_e4m3fn_x4

RELU = mybir.ActivationFunctionType.Relu
SQUARE = mybir.ActivationFunctionType.Square
MULT, ADD = mybir.AluOpType.mult, mybir.AluOpType.add

CHUNKS = ((0, 3), (3, 3), (6, 2))
HALF = 512
RAW_BUFS = 8
AHEAD = 6
UNITS = ((0, 0, 1024), (1, 0, 640), (1, 640, 1024))


def tile_moe_shr_lin_relu2_kernel(tc, xT, w, b, gate, offs, pos1, pos2, out):
    nc = tc.nc
    with ExitStack() as ctx:
        lists = ctx.enter_context(tc.tile_pool(name="lists", bufs=1))
        keep = ctx.enter_context(tc.tile_pool(name="keep", bufs=1))
        stage = ctx.enter_context(tc.tile_pool(name="stage", bufs=RAW_BUFS))
        group = ctx.enter_context(tc.tile_pool(name="group", bufs=1))
        psum = ctx.enter_context(tc.psum_pool(name="psum", bufs=8))

        offs_t = lists.tile([P, S // 16], U16, name="offs_t")
        pos1_t = lists.tile([P, T // 16], U16, name="pos1_t")
        pos2_t = lists.tile([P, T // 16], U16, name="pos2_t")
        pos = (pos1_t, pos2_t)

        bias = keep.tile([P, 2, E + 1], F32, name="bias")
        plane0 = keep.tile([P, T], U32, name="plane0")
        plane1 = keep.tile([P, T], U32, name="plane1")
        planes23 = keep.tile([P, 2, T], U32, name="planes23")
        planes = (plane0[:], plane1[:], planes23[:, 0, :], planes23[:, 1, :])
        picked = [keep.tile([P, 4, n * C], U32, name=f"picked{i}") for i, (e0, n) in enumerate(CHUNKS)]
        y = [keep.tile([P, S], F32, name=f"y{m}") for m in range(2)]
        ys = [keep.tile([P, T], F32, name=f"ys{m}") for m in range(2)]
        wcodes = [keep.tile([P, 4 * N], U32, name=f"wcodes{k}", align_bytes=64) for k in range(E // 2)]
        wscales = [keep.tile([P, 4 * N], U8, name=f"wscales{k}", align_bytes=64) for k in range(E // 2)]
        wcodes.append(keep.tile([P, 2 * N], U32, name="wcodes8", align_bytes=64))
        wscales.append(keep.tile([P, 2 * N], U8, name="wscales8", align_bytes=64))
        scodes = [keep.tile([P, T], U32, name=f"scodes{g}", align_bytes=64) for g in range(2)]
        sscales = [keep.tile([P, T], U8, name=f"sscales{g}", align_bytes=64) for g in range(2)]

        nc.sync.dma_start(offs_t[:], offs)
        rows = [xT[HALF * g : HALF * (g + 1), :].rearrange("(p j) t -> p j t", j=4) for g in range(2)]
        raw01 = []
        for h in range(2):
            t = stage.tile([P, 2048], F32, name="raw")
            raw01.append(t[:].rearrange("p (j t) -> p j t", j=4))
        for q in range(2):
            for h in range(2):
                cols = slice(h * HALF, (h + 1) * HALF)
                nc.sync.dma_start(raw01[h][:, 2 * q : 2 * q + 2, :], rows[0][:, 2 * q : 2 * q + 2, cols])

        ring = [("x", 2), ("x", 3)] + [("w", e) for e in range(E + 1)] + [("gate", 0), ("gate", 1)]
        raw = {}

        def load(unit):
            kind, j = unit
            t = stage.tile([P, 2048], F32, name="raw")
            raw[unit] = t
            if kind == "x":
                nc.sync.dma_start(t[:].rearrange("p (j t) -> p j t", j=2), rows[1][:, 2 * j - 4 : 2 * j - 2, :])
            elif kind == "w":
                nc.sync.dma_start(
                    t[:].rearrange("p (g j n) -> p g j n", g=2, j=4),
                    w[j].rearrange("(g p j) n -> p g j n", p=P, j=4),
                )
            else:
                nc.sync.dma_start(
                    t[:].rearrange("p (r t) -> p r t", r=2),
                    gate[:, j * P : (j + 1) * P, :].rearrange("r p t -> p r t"),
                )
            if unit == ("w", E):
                nc.sync.dma_start(bias[:], b.rearrange("(m p) e -> p m e", p=P))
            if unit == ("w", 2):
                nc.sync.dma_start(pos1_t[:], pos1)
                nc.sync.dma_start(pos2_t[:], pos2)

        def load_ahead(unit):
            for u in ring[: ring.index(unit) + AHEAD]:
                if u not in raw:
                    load(u)

        def cast_plane(q):
            dst = planes[q].bitcast(BF16).rearrange("p (t e) -> p t e", e=2)
            if q < 2:
                for h in range(2):
                    half = dst[:, h * HALF : (h + 1) * HALF, :]
                    src = raw01[h][:, 2 * q : 2 * q + 2, :].rearrange("p e t -> p t e")
                    if q == 0:
                        nc.vector.tensor_copy(half, src)
                    else:
                        nc.scalar.copy(half, src)
            else:
                load_ahead(("x", q))
                nc.scalar.copy(dst, raw[("x", q)][:].rearrange("p (e t) -> p t e", e=2))

        wbf = {}

        def cast_w(e):
            load_ahead(("w", e))
            if e in (6, 7):
                if e == 6:
                    t = group.tile([P, 16 * N], BF16, name="tail", align_bytes=64)
                    wbf[3] = t
            elif e % 2 == 0:
                t = group.tile([P, 16 * N], BF16, name="wbf", align_bytes=64, bufs=3)
                wbf[e // 2] = t
            for g in range(2):
                src = raw[("w", e)][:, 4 * N * g : 4 * N * (g + 1)].rearrange("p (j c i) -> p c j i", j=4, i=4)
                c0 = 8 * N * (e % 2) + 4 * N * g
                dst = wbf[e // 2][:, c0 : c0 + 4 * N].rearrange("p (c i j) -> p c j i", i=4, j=4)
                nc.scalar.copy(dst, src)

        def quant_w(k):
            n = 4 * N if k < E // 2 else 2 * N
            nc.vector.quantize_mx(out=wcodes[k][:].bitcast(FP8X4), scales=wscales[k][:], in_=wbf[k][:, 0 : 4 * n])

        def gather(q, chunks=(0, 1, 2)):
            for i in chunks:
                e0, n = CHUNKS[i]
                nc.vector.tensor_copy(picked[i][:, q, :], planes[q].indirect(offs_t[:, 16 * e0 : 16 * (e0 + n)]))

        xbf, xcodes, xscales = {}, {}, {}

        def group_x(i, g):
            n = CHUNKS[i][1] * C
            if g == 0:
                t = group.tile([P, 8 * n], BF16, name="xbf", align_bytes=64)
                xbf[i] = t
            src = picked[i][:, 2 * g : 2 * g + 2, :].bitcast(BF16).rearrange("p h (c e) -> p c h e", e=2)
            nc.vector.tensor_copy(xbf[i][:, 4 * n * g : 4 * n * (g + 1)].rearrange("p (c h e) -> p c h e", h=2, e=2), src)

        def quant_x(i):
            n = CHUNKS[i][1] * C
            xc = group.tile([P, 2 * n], U32, name="xc", align_bytes=64, bufs=2)
            xs = group.tile([P, 2 * n], U8, name="xs", align_bytes=64, bufs=2)
            xcodes[i], xscales[i] = xc, xs
            for c0 in range(0, 2 * n, 1024):
                c1 = min(c0 + 1024, 2 * n)
                nc.vector.quantize_mx(out=xc[:, c0:c1].bitcast(FP8X4), scales=xs[:, c0:c1], in_=xbf[i][:, 4 * c0 : 4 * c1])

        banks = {}

        def multiply(k):
            for e in (2 * k, 2 * k + 1):
                ps = psum.tile([P, 2 * C], F32, name="ps")
                banks[e] = ps
            for m in range(2):
                for e in (2 * k, 2 * k + 1):
                    i = min(e // 3, 2)
                    e0, n = CHUNKS[i]
                    for g in range(2):
                        w0 = 2 * N * (e % 2) + N * g + P * m
                        x0 = C * (n * g + e - e0)
                        nc.tensor.matmul_mx(
                            out=banks[e][:, C * m : C * (m + 1)],
                            lhsT=wcodes[k][:, w0 : w0 + P].bitcast(FP8X4),
                            lhsT_scale=wscales[k][:, w0 : w0 + P],
                            rhs=xcodes[i][:, x0 : x0 + C].bitcast(FP8X4),
                            rhs_scale=xscales[i][:, x0 : x0 + C],
                            start=(g == 0),
                            stop=(g == 1),
                        )

        def relu(k, m):
            for e in (2 * k, 2 * k + 1):
                v = y[m][:, C * e : C * (e + 1)]
                nc.scalar.activation(v, banks[e][:, C * m : C * (m + 1)], RELU, bias=bias[:, m, e : e + 1])

        def square(k, m):
            v = y[m][:, 2 * C * k : 2 * C * (k + 1)]
            nc.scalar.activation(v, v, SQUARE)

        sbf = {}

        def group_s(g, h=0):
            if g == 0:
                t = group.tile([P, 4 * HALF], BF16, name="sbf", align_bytes=64, bufs=2)
                src = raw01[h].rearrange("p j (c i) -> p c j i", i=4)
                dst = t[:].rearrange("p (c i j) -> p c j i", i=4, j=4)
                nc.scalar.copy(dst, src)
            else:
                t = group.tile([P, 4 * T], BF16, name="tail", align_bytes=64)
                src = planes23[:].bitcast(BF16).rearrange("p q (c e) -> p c q e", e=2)
                nc.vector.tensor_copy(t[:].rearrange("p (c q e) -> p c q e", q=2, e=2), src)
            sbf[(g, h)] = t

        def quant_s(g, h=0):
            cols = slice(h * HALF, (h + 1) * HALF) if g == 0 else slice(0, T)
            nc.vector.quantize_mx(out=scodes[g][:, cols].bitcast(FP8X4), scales=sscales[g][:, cols], in_=sbf[(g, h)][:])

        def shared(m, h):
            ps = psum.tile([P, HALF], F32, name="ps")
            for g in range(2):
                w0 = N * g + P * m
                nc.tensor.matmul_mx(
                    out=ps[:],
                    lhsT=wcodes[E // 2][:, w0 : w0 + P].bitcast(FP8X4),
                    lhsT_scale=wscales[E // 2][:, w0 : w0 + P],
                    rhs=scodes[g][:, HALF * h : HALF * (h + 1)].bitcast(FP8X4),
                    rhs_scale=sscales[g][:, HALF * h : HALF * (h + 1)],
                    start=(g == 0),
                    stop=(g == 1),
                )
            v = ys[m][:, HALF * h : HALF * (h + 1)]
            nc.scalar.activation(v, ps[:], RELU, bias=bias[:, m, E : E + 1])

        def square_shared(m, h):
            v = ys[m][:, HALF * h : HALF * (h + 1)]
            nc.scalar.activation(v, v, SQUARE)

        part = {}

        def fetch(u, r):
            m, c0, c1 = UNITS[u]
            if r == 0:
                t = stage.tile([P, 2048], F32, name="raw")
                part[u] = t[:].rearrange("p (r c) -> p r c", r=2)
            weight = raw[("gate", m)][:, T * r + c0 : T * r + c1]
            nc.vector.tensor_tensor(
                part[u][:, r, 0 : c1 - c0], y[m][:].indirect(pos[r][:, c0 // 16 : c1 // 16]), weight, MULT
            )

        def add_parts(u):
            m, c0, c1 = UNITS[u]
            v = part[u][:, :, 0 : c1 - c0]
            nc.vector.tensor_tensor(v[:, 0], v[:, 0], v[:, 1], ADD)

        def finish(u):
            m, c0, c1 = UNITS[u]
            v = part[u][:, 0, 0 : c1 - c0]
            nc.vector.tensor_tensor(v, v, ys[m][:, c0:c1], ADD)
            nc.sync.dma_start(out[m * P : (m + 1) * P, c0:c1], v)

        cast_plane(0)
        cast_plane(1)
        group_s(0, 0)
        gather(0)
        cast_plane(2)
        cast_plane(3)
        group_s(0, 1)
        cast_w(0)
        gather(1)
        cast_w(1)
        gather(2)
        cast_w(2)
        gather(3)
        for e in range(3, E):
            cast_w(e)
        group_x(0, 0)
        group_x(0, 1)
        quant_s(0, 0)
        quant_x(0)
        group_x(1, 0)
        quant_s(0, 1)
        group_x(1, 1)
        quant_w(0)
        cast_w(E)
        load_ahead(ring[-1])
        quant_x(1)
        multiply(0)
        relu(0, 0)
        quant_w(1)
        multiply(1)
        relu(1, 0)
        square(0, 0)
        quant_w(2)
        multiply(2)
        relu(2, 0)
        square(1, 0)
        square(2, 0)
        group_x(2, 0)
        group_x(2, 1)
        quant_w(3)
        quant_x(2)
        multiply(3)
        relu(3, 0)
        square(3, 0)
        relu(0, 1)
        relu(1, 1)
        square(0, 1)
        relu(2, 1)
        square(1, 1)
        relu(3, 1)
        square(2, 1)
        square(3, 1)
        group_s(1)
        quant_w(4)
        fetch(0, 0)
        quant_s(1)
        fetch(0, 1)
        for m in range(2):
            shared(m, 0)
            shared(m, 1)
            square_shared(m, 0)
            square_shared(m, 1)
        add_parts(0)
        fetch(1, 0)
        fetch(1, 1)
        finish(0)
        fetch(2, 0)
        add_parts(1)
        fetch(2, 1)
        finish(1)
        add_parts(2)
        finish(2)
